import numpy as np
import ml_dtypes


def mxq(x, axis, fmt="e4m3"):
    dtype, down = {"e4m3": (ml_dtypes.float8_e4m3fn, 7), "e5m2": (ml_dtypes.float8_e5m2, 14)}[fmt]
    v = np.moveaxis(np.asarray(x, np.float32).astype(ml_dtypes.bfloat16).astype(np.float64), axis, -1)
    blocks = v.reshape(v.shape[:-1] + (-1, 32))
    amax = np.abs(blocks).max(-1, keepdims=True)
    byte = np.maximum(np.where(amax > 0, np.frexp(amax)[1] - 1 + 127, 0) - down, 1)
    scale = np.exp2(byte - 127.0)
    codes = (blocks / scale).astype(np.float32).astype(dtype).astype(np.float64)
    return np.moveaxis((codes * scale).reshape(v.shape), -1, axis)


WIDE = False


def mx_kscale(k):
    if not WIDE:
        return np.ones(k)
    levels = np.array([10, -10, 5, -5, 0])
    if k % 512:
        return np.exp2(np.random.permutation(np.resize(levels, k // 32))).repeat(32)
    a = np.empty((k // 512, 16))
    for p in range(k // 512):
        a[p, :8] = np.random.permutation(np.resize(levels, 8))
        for g in range(8):
            far = levels[np.abs(levels - a[p, g]) >= 10]
            a[p, g + 8] = far[np.random.randint(len(far))]
    return np.exp2(a.ravel()).repeat(32)


BF16 = ml_dtypes.bfloat16


def bf(x):
    return np.asarray(x, np.float32).astype(BF16)


def f64(x):
    return np.asarray(x).astype(np.float64)


E2M1 = np.array([0.0, 0.5, 1.0, 1.5, 2.0, 3.0, 4.0, 6.0, -0.0, -0.5, -1.0, -1.5, -2.0, -3.0, -4.0, -6.0])


def pack_weight(w, fmt):
    k, n = w.shape
    w = f64(bf(w)).reshape(k // 32, 32, n)
    amax = np.abs(w).max(1)
    if fmt == "e4m3":
        byte = np.frexp(amax)[1] - 1 + 127 - 7
    else:
        mant, ex = np.frexp(amax / 6.0)
        byte = np.where(mant > 0.5, ex, ex - 1) + 127
    byte = np.clip(np.where(amax > 0, byte, 1), 1, 254)
    scaled = (w * np.exp2(127.0 - byte)[:, None, :]).reshape(k, n).astype(np.float32)
    by_word = np.ascontiguousarray(scaled.reshape(k // 512, 128, 4, n).transpose(0, 1, 3, 2))
    if fmt == "e4m3":
        words = by_word.astype(ml_dtypes.float8_e4m3fn).view(np.uint8)
    else:
        c = by_word.astype(ml_dtypes.float4_e2m1fn).view(np.uint8) & 0xF
        words = c[..., 0::2] | (c[..., 1::2] << 4)
    return np.ascontiguousarray(words), np.ascontiguousarray(byte.astype(np.uint8).reshape(k // 512, 16, n))


def unpack_weight(words, scales, fmt):
    g, p, n, _ = words.shape
    if fmt == "e4m3":
        vals = np.ascontiguousarray(words).view(ml_dtypes.float8_e4m3fn).astype(np.float64)
    else:
        nib = np.empty((g, p, n, 4), np.uint8)
        nib[..., 0::2] = words & 0xF
        nib[..., 1::2] = words >> 4
        vals = E2M1[nib]
    vals = vals * np.repeat(np.exp2(scales.astype(np.float64) - 127.0), 8, axis=1)[..., None]
    return vals.transpose(0, 1, 3, 2).reshape(g * 512, n)
def pack4(w):
    words, scales = pack_weight(w, "e2m1")
    return words.reshape(words.shape[0], 128, -1), scales


def unpack4(words, scales):
    return unpack_weight(words.reshape(words.shape[0], 128, -1, 2), scales, "e2m1")


def planes(Y):
    n, m = Y.shape
    b = f64(bf(Y)).reshape(n // 32, 32, m)
    amax = np.abs(b).max(1)
    byte = np.clip(np.where(amax > 0, np.frexp(amax)[1] - 1 + 127 - 7, 1), 1, 254)
    codes = (b * np.exp2(127.0 - byte)[:, None, :]).reshape(n, m).astype(np.float32).astype(ml_dtypes.float8_e4m3fn).view(np.uint8)
    words = codes.reshape(n // 512, 128, 4, m).transpose(0, 1, 3, 2)
    return np.ascontiguousarray(words), np.ascontiguousarray(byte.astype(np.uint8).reshape(n // 512, 16, m))


N, D, F, C = 1024, 1024, 1024, 512


def sigmoid(x):
    return 1.0 / (1.0 + np.exp(-x))


def setup_inputs():
    sd, t = mx_kscale(D), mx_kscale(F)
    v1 = bf(np.random.standard_normal((N, D)) * sd)
    v2 = bf(np.random.standard_normal((N, F)))
    s = bf(np.random.standard_normal(N))
    a = bf(np.random.standard_normal(D) * sd)
    w_words, w_scales = pack4(np.random.standard_normal((D, F)) / np.sqrt(D) / sd[:, None])
    g = bf((1.0 + 0.1 * np.random.standard_normal(F)) * t)
    wy_words, wy_scales = pack4(np.random.standard_normal((F, C)) * 1.5 / np.sqrt(F) / t[:, None])
    return {
        "v1": v1,
        "v2": v2,
        "s": s,
        "a": a,
        "w_words": w_words,
        "w_scales": w_scales,
        "g": g,
        "wy_words": wy_words,
        "wy_scales": wy_scales,
    }


def flip_first_stage(v1, s, a):
    return v1 - 2.0 * s[:, None] * a[None, :]


def predict(v, g, wyq):
    return sigmoid(mxq(v * g[None, :], 1, "e4m3") @ wyq)


def core(v1, v2, s, a, w_words, w_scales, g, wy_words, wy_scales):
    v1, v2, s, a, g = f64(v1), f64(v2), f64(s), f64(a), f64(g)
    wq = unpack4(w_words, w_scales)
    wyq = unpack4(wy_words, wy_scales)
    v1c = flip_first_stage(v1, s, a)
    h = np.tanh(mxq(v1, 1, "e4m3") @ wq)
    hc = np.tanh(mxq(v1c, 1, "e4m3") @ wq)
    v2c = v2 - h + hc
    p = predict(v2, g, wyq)
    pc = predict(v2c, g, wyq)
    return pc - p


def reference(v1, v2, s, a, w_words, w_scales, g, wy_words, wy_scales):
    R_out = core(v1, v2, s, a, w_words, w_scales, g, wy_words, wy_scales)
    words, scales = planes(R_out)
    return R_out, words, scales

@@ -1,0 +1,357 @@
+from contextlib import ExitStack
+
+import concourse.mybir as mybir
+from concourse.masks import make_identity
+
+F32 = mybir.dt.float32
+BF16 = mybir.dt.bfloat16
+I32 = mybir.dt.int32
+U32 = mybir.dt.uint32
+U8 = mybir.dt.uint8
+FP8X4 = mybir.dt.float8_e4m3fn_x4
+FP4X4 = mybir.dt.float4_e2m1fn_x4
+ALU = mybir.AluOpType
+ACT = mybir.ActivationFunctionType
+
+N, D, F, C = 1024, 1024, 1024, 512
+P = 128
+NT = N // P
+FLOPS = 2 * (2 * N * D * F) + 2 * (2 * N * F * C)
+
+
+def tile_counterfactualfairnessabductiongap_x2_kernel(
+    tc, v1, v2, s, a, w_words, w_scales, g, wy_words, wy_scales, out_0, out_1, out_2
+):
+    nc = tc.nc
+    with ExitStack() as ctx:
+        keep = ctx.enter_context(tc.tile_pool(name="keep", bufs=1))
+        inp = ctx.enter_context(tc.tile_pool(name="inp", bufs=NT))
+        ahead = ctx.enter_context(tc.tile_pool(name="ahead", bufs=6))
+        work = ctx.enter_context(tc.tile_pool(name="work", bufs=3))
+        res = ctx.enter_context(tc.tile_pool(name="res", bufs=2))
+        tp_pool = ctx.enter_context(tc.psum_pool(name="tp", bufs=3))
+        m1_pool = ctx.enter_context(tc.psum_pool(name="m1", bufs=3))
+        m2_pool = ctx.enter_context(tc.psum_pool(name="m2", bufs=2))
+        ctx.enter_context(tc.manual_schedule())
+
+        ident = keep.tile([P, P], F32, name="ident")
+        ident_bf = keep.tile([P, P], BF16, name="ident_bf")
+        w_sb = keep.tile([P, 2, 2 * F], U8, name="w_sb", align_bytes=64)
+        w_sc = keep.tile([P, 2, F], U8, name="w_sc", align_bytes=64)
+        wy_sb = keep.tile([P, 2, 2 * C], U8, name="wy_sb", align_bytes=64)
+        wy_sc = keep.tile([P, 2, C], U8, name="wy_sc", align_bytes=64)
+        a_col = keep.tile([P, 2, 4], BF16, name="a_col")
+        g_col = keep.tile([P, 2, 4], BF16, name="g_col")
+        s_col = keep.tile([P, 2, 4], BF16, name="s_col")
+        m2s = keep.tile([P, NT], F32, name="m2s")
+        a_b = keep.tile([P, D], BF16, name="a_b", align_bytes=64)
+        g_b = keep.tile([P, F], BF16, name="g_b", align_bytes=64)
+        warm = keep.tile([P, 1], F32, name="warm")
+
+        v1_rows = v1.rearrange("(g m t) d -> g t m d", m=P, t=4)
+        v2_rows = v2.rearrange("(g m t) d -> g t m d", m=P, t=4)
+        out_rows = out_0.rearrange("(g m t) c -> g t m c", m=P, t=4)
+
+        make_identity(nc, ident_bf[:])
+        make_identity(nc, ident[:])
+        nc.vector.memset(w_sc[:].rearrange("p g n -> p (g n)").bitcast(I32), 0)
+        nc.vector.memset(wy_sc[:].rearrange("p g n -> p (g n)").bitcast(I32), 0)
+
+        for col, src in ((a_col, a), (s_col, s), (g_col, g)):
+            nc.scalar.dma_start(out=col[:], in_=src.rearrange("(g p t) -> p g t", p=P, t=4))
+        nc.vector.memset(warm[:], 0.0)
+        nc.scalar.activation(out=warm[:], in_=warm[:], func=ACT.Sigmoid)
+
+        v1_sb, v2_sb = [], []
+        for i in range(NT):
+            v1_sb.append(inp.tile([P, D], BF16, name="v1_t", align_bytes=64))
+            v2_sb.append(inp.tile([P, F], BF16, name="v2_t", align_bytes=64))
+
+        def load_v1(i):
+            nc.sync.dma_start(out=v1_sb[i][:], in_=v1_rows[i // 4, i % 4])
+
+        def load_v2(i):
+            nc.sync.dma_start(out=v2_sb[i][:], in_=v2_rows[i // 4, i % 4])
+
+        def load_weight(words_sb, scales_sb, words, scales):
+            rows = scales.bitcast(I32)
+            plane = scales_sb[:].bitcast(I32)
+            for q in range(4):
+                nc.sync.dma_start(
+                    out=plane[32 * q : 32 * q + 4],
+                    in_=rows[:, 4 * q : 4 * q + 4, :].rearrange("g r n -> r g n"),
+                )
+            for k in range(2):
+                nc.sync.dma_start(out=words_sb[:, k, :].bitcast(I32), in_=words[k].bitcast(I32))
+
+        load_v1(0)
+        load_v1(1)
+        load_weight(w_sb, w_sc, w_words, w_scales)
+        load_v2(0)
+        load_v1(2)
+        load_v1(3)
+        load_v2(1)
+        load_v1(4)
+        load_v2(2)
+        load_weight(wy_sb, wy_sc, wy_words, wy_scales)
+        load_v1(5)
+        load_v2(3)
+        load_v1(6)
+        load_v2(4)
+        load_v1(7)
+        for i in range(5, NT):
+            load_v2(i)
+
+        nc.vector.tensor_scalar(
+            out=m2s[:], in0=s_col[:].rearrange("p g t -> p (g t)"), scalar1=-2.0, scalar2=None, op0=ALU.mult
+        )
+
+        def spread(col, full, copy):
+            bank = tp_pool.tile([P, NT, P], BF16, name="spread", tag="tp")
+            flat = col[:].rearrange("p g t -> p (g t)")
+            for j in range(8):
+                nc.tensor.transpose(bank[:, j, :], flat[:, j : j + 1].to_broadcast([P, P]), ident_bf[:])
+            copy(
+                out=full[:].rearrange("p (g n t) -> p g n t", g=2, t=4),
+                in_=bank[:].rearrange("p (g t) n -> p g n t", g=2),
+            )
+
+        spread(a_col, a_b, nc.vector.tensor_copy)
+        spread(g_col, g_b, nc.scalar.copy)
+
+        st = [dict() for i in range(NT)]
+        groups = [dict(), dict()]
+
+        def stt(i):
+            t = ahead.tile([P, D], BF16, name="v1c", align_bytes=64)
+            nc.vector.scalar_tensor_tensor(
+                out=t[:], in0=a_b[:], scalar=m2s[:, i : i + 1], in1=v1_sb[i][:], op0=ALU.mult, op1=ALU.add
+            )
+            st[i]["v1c"] = t
+
+        def turn(src, ks):
+            words = src[:].bitcast(F32)
+            bank = tp_pool.tile([P, len(ks), 2, P], F32, name="turned", tag="tp")
+            for j, k in enumerate(ks):
+                for u in range(2):
+                    nc.tensor.transpose(bank[:, j, u, :], words[:, 256 * k + u : 256 * (k + 1) : 2], ident[:])
+            return bank
+
+        def unload(bank, dst):
+            k = dst.shape[1]
+            nc.scalar.copy(
+                out=dst.rearrange("p g n t -> p (g n t)").bitcast(F32).rearrange("p (g n u) -> p g n u", g=k, u=2),
+                in_=bank[:].rearrange("p g u n -> p g n u"),
+            )
+
+        def tp1(i):
+            st[i]["b1"] = turn(v1_sb[i], (0, 1))
+
+        def tp1c(i):
+            st[i]["b1c"] = turn(st[i]["v1c"], (0, 1))
+
+        def tp2(i):
+            st[i]["b2"] = turn(v2_sb[i], (0, 1))
+
+        def vt(i):
+            if "vt" not in st[i]:
+                st[i]["vt"] = work.tile([P, 2, 2, P, 4], BF16, name="vt", align_bytes=64)
+            return st[i]["vt"]
+
+        def ut(i):
+            if "ut" not in st[i]:
+                st[i]["ut"] = work.tile([P, 2, 2, P, 4], BF16, name="ut", align_bytes=64)
+                st[i]["uq"] = work.tile([P, 4 * P], U32, name="uq", align_bytes=64)
+                st[i]["us"] = work.tile([P, 4 * P], U8, name="us", align_bytes=64)
+            return st[i]["ut"]
+
+        def ev1(i):
+            unload(st[i]["b1"], vt(i)[:, 0])
+
+        def ev1c(i):
+            unload(st[i]["b1c"], vt(i)[:, 1])
+
+        def quant(codes, scales, src):
+            nc.vector.quantize_mx(out=codes.bitcast(FP8X4), scales=scales, in_=src)
+
+        def q1(i):
+            st[i]["vq"] = work.tile([P, 4 * P], U32, name="vq", align_bytes=64)
+            st[i]["vs"] = work.tile([P, 4 * P], U8, name="vs", align_bytes=64)
+            quant(st[i]["vq"][:], st[i]["vs"][:], vt(i)[:].rearrange("p w g n t -> p (w g n t)"))
+
+        def mx(bank, codes, scales, first, words, wscales, half):
+            for k in range(2):
+                cols = slice((first + k) * P, (first + k + 1) * P)
+                nc.tensor.matmul_mx(
+                    out=bank[:],
+                    lhsT=codes[:, cols].bitcast(FP8X4),
+                    lhsT_scale=scales[:, cols],
+                    rhs=words[:, k, 1024 * half : 1024 * (half + 1)].bitcast(FP4X4),
+                    rhs_scale=wscales[:, k, 512 * half : 512 * (half + 1)],
+                    start=(k == 0),
+                    stop=(k == 1),
+                )
+
+        def m1(i, which, half):
+            bank = m1_pool.tile([P, 512], F32, name="m1", tag="m1")
+            mx(bank, st[i]["vq"], st[i]["vs"], 2 * which, w_sb, w_sc, half)
+            st[i]["m1", which, half] = bank
+
+        def tanh(i, which, half):
+            key = "hc" if which else "h"
+            if key not in st[i]:
+                st[i][key] = work.tile([P, F], F32, name=key)
+            nc.scalar.activation(
+                out=st[i][key][:, 512 * half : 512 * (half + 1)], in_=st[i]["m1", which, half][:], func=ACT.Tanh
+            )
+
+        def pieces(i):
+            return ((0, 512), (512, 1024)) if i == NT - 1 else ((0, 1024),)
+
+        def d_op(i):
+            st[i]["e"] = work.tile([P, F], F32, name="e")
+            for lo, hi in pieces(i):
+                nc.vector.tensor_tensor(
+                    out=st[i]["e"][:, lo:hi], in0=st[i]["hc"][:, lo:hi], in1=st[i]["h"][:, lo:hi], op=ALU.subtract
+                )
+
+        def e_op(i):
+            for lo, hi in pieces(i):
+                e = st[i]["e"][:, lo:hi]
+                nc.vector.tensor_tensor(out=e, in0=e, in1=v2_sb[i][:, lo:hi], op=ALU.add)
+
+        def x_op(i):
+            st[i]["uc"] = work.tile([P, F], BF16, name="uc", align_bytes=64)
+            for lo, hi in pieces(i):
+                nc.vector.tensor_tensor(
+                    out=st[i]["uc"][:, lo:hi], in0=st[i]["e"][:, lo:hi], in1=g_b[:, lo:hi], op=ALU.mult
+                )
+
+        def u_op(i):
+            dst = ut(i)
+            turned = st[i]["b2"][:].rearrange("p g u n -> p (g u n)").bitcast(BF16)
+            turned = turned.rearrange("p (g u n e) -> p g n u e", g=2, u=2, e=2)
+            for k in range(2):
+                gain = g_col[:, k, :].rearrange("p (u e) -> p u e", e=2).unsqueeze(1).to_broadcast([P, P, 2, 2])
+                nc.vector.tensor_tensor(
+                    out=dst[:, 0, k].rearrange("p n (u e) -> p n u e", e=2), in0=turned[:, k], in1=gain, op=ALU.mult
+                )
+            if i == NT - 1:
+                quant(st[i]["uq"][:, 0 : 2 * P], st[i]["us"][:, 0 : 2 * P], dst[:, 0].rearrange("p g n t -> p (g n t)"))
+
+        def tp3(i):
+            if i == NT - 1:
+                st[i]["b3"] = [turn(st[i]["uc"], (k,)) for k in range(2)]
+            else:
+                st[i]["b3"] = [turn(st[i]["uc"], (0, 1))]
+
+        def ev3(i):
+            dst = ut(i)
+            if i == NT - 1:
+                for k in range(2):
+                    unload(st[i]["b3"][k], dst[:, 1, k : k + 1])
+            else:
+                unload(st[i]["b3"][0], dst[:, 1])
+
+        def q2(i):
+            t = ut(i)
+            if i == NT - 1:
+                for k in range(2):
+                    cols = slice((2 + k) * P, (3 + k) * P)
+                    quant(st[i]["uq"][:, cols], st[i]["us"][:, cols], t[:, 1, k].rearrange("p n t -> p (n t)"))
+            else:
+                quant(st[i]["uq"][:], st[i]["us"][:], t[:].rearrange("p w g n t -> p (w g n t)"))
+
+        def m2(i, which):
+            bank = m2_pool.tile([P, C], F32, name="m2", tag="m2")
+            mx(bank, st[i]["uq"], st[i]["us"], 2 * which, wy_sb, wy_sc, 0)
+            st[i]["m2", which] = bank
+
+        def halves(i):
+            return ((0, 256), (256, 512)) if i == NT - 1 else ((0, 512),)
+
+        def sig(i, which):
+            st[i]["p", which] = work.tile([P, C], F32, name="pc" if which else "p")
+            for lo, hi in halves(i) if which else ((0, C),):
+                nc.scalar.activation(
+                    out=st[i]["p", which][:, lo:hi], in_=st[i]["m2", which][:, lo:hi], func=ACT.Sigmoid
+                )
+
+        def df(i):
+            grp = groups[i // 4]
+            if "r" not in grp:
+                grp["r"] = res.tile([P, 4, C], F32, name="r")
+                grp["pb"] = res.tile([P, C, 4], BF16, name="pb", align_bytes=64)
+                grp["q"] = res.tile([P, C], U32, name="rq", align_bytes=64)
+                grp["s"] = res.tile([P, C], U8, name="rs", align_bytes=64)
+            for lo, hi in halves(i):
+                r = grp["r"][:, i % 4, lo:hi]
+                nc.vector.tensor_tensor(
+                    out=r, in0=st[i]["p", 1][:, lo:hi], in1=st[i]["p", 0][:, lo:hi], op=ALU.subtract
+                )
+                nc.sync.dma_start(out=out_rows[i // 4, i % 4][:, lo:hi], in_=r)
+
+        def pack(G, lo, hi, copy):
+            grp = groups[G]
+            copy(out=grp["pb"][:, lo:hi, :], in_=grp["r"][:, :, lo:hi].rearrange("p t c -> p c t"))
+
+        def plane_words(G, lo, hi):
+            grp = groups[G]
+            quant(grp["q"][:, lo:hi], grp["s"][:, lo:hi], grp["pb"][:, lo:hi, :].rearrange("p c t -> p (c t)"))
+            nc.sync.dma_start(
+                out=out_1[G].rearrange("p m t -> p (m t)").bitcast(I32)[:, lo:hi], in_=grp["q"][:, lo:hi].bitcast(I32)
+            )
+
+        def plane_scales(G):
+            for q in range(4):
+                nc.sync.dma_start(
+                    out=out_2[G, 4 * q : 4 * q + 4, :].bitcast(I32),
+                    in_=groups[G]["s"][32 * q : 32 * q + 4, :].bitcast(I32),
+                )
+
+        for k in range(-4, NT + 4):
+
+            def at(offset, op, *args):
+                if 0 <= k - offset < NT:
+                    op(k - offset, *args)
+
+            at(-1, ev1c)
+            at(1, tanh, 1, 0)
+            at(4, m2, 0)
+            at(4, sig, 0)
+            at(1, m1, 0, 0)
+            at(3, tp3)
+            at(3, ev3)
+            at(0, q1)
+            at(2, e_op)
+            at(-4, stt)
+            at(3, q2)
+            at(2, x_op)
+            at(1, tanh, 0, 0)
+            at(1, m1, 1, 1)
+            at(1, tanh, 1, 1)
+            at(1, m1, 0, 1)
+            at(1, tanh, 0, 1)
+            at(4, m2, 1)
+            at(4, sig, 1)
+            at(4, df)
+            at(1, d_op)
+            at(-1, tp1)
+            at(-1, ev1)
+            at(2, tp2)
+            at(2, u_op)
+            at(-2, tp1c)
+            at(0, m1, 1, 0)
+            if k in (8, 9):
+                pack(0, 256 * (k - 8), 256 * (k - 8) + 128, nc.scalar.copy)
+                pack(0, 256 * (k - 8) + 128, 256 * (k - 8) + 256, nc.scalar.copy)
+            if k == 10:
+                plane_words(0, 0, C)
+                plane_scales(0)
+        pack(1, 0, 128, nc.scalar.copy)
+        pack(1, 384, 512, nc.scalar.copy)
+        pack(1, 128, 256, nc.vector.tensor_copy)
+        plane_words(1, 0, 256)
+        pack(1, 256, 384, nc.vector.tensor_copy)
+        plane_words(1, 256, 512)
+        plane_scales(1)

@@ -27,7 +27,7 @@ def tile_counterfactualfairnessabductiongap_x2_kernel(
         keep = ctx.enter_context(tc.tile_pool(name="keep", bufs=1))
         inp = ctx.enter_context(tc.tile_pool(name="inp", bufs=NT))
         ahead = ctx.enter_context(tc.tile_pool(name="ahead", bufs=6))
-        work = ctx.enter_context(tc.tile_pool(name="work", bufs=3))
+        work = ctx.enter_context(tc.tile_pool(name="work", bufs=4))
         res = ctx.enter_context(tc.tile_pool(name="res", bufs=2))
         tp_pool = ctx.enter_context(tc.psum_pool(name="tp", bufs=3))
         m1_pool = ctx.enter_context(tc.psum_pool(name="m1", bufs=3))
@@ -57,8 +57,8 @@ def tile_counterfactualfairnessabductiongap_x2_kernel(
         nc.vector.memset(w_sc[:].rearrange("p g n -> p (g n)").bitcast(I32), 0)
         nc.vector.memset(wy_sc[:].rearrange("p g n -> p (g n)").bitcast(I32), 0)
 
-        for col, src in ((a_col, a), (s_col, s), (g_col, g)):
-            nc.scalar.dma_start(out=col[:], in_=src.rearrange("(g p t) -> p g t", p=P, t=4))
+        for queue, col, src in ((nc.sync, a_col, a), (nc.scalar, s_col, s), (nc.scalar, g_col, g)):
+            queue.dma_start(out=col[:], in_=src.rearrange("(g p t) -> p g t", p=P, t=4))
         nc.vector.memset(warm[:], 0.0)
         nc.scalar.activation(out=warm[:], in_=warm[:], func=ACT.Sigmoid)
 
@@ -151,7 +151,7 @@ def tile_counterfactualfairnessabductiongap_x2_kernel(
             st[i]["b1c"] = turn(st[i]["v1c"], (0, 1))
 
         def tp2(i):
-            st[i]["b2"] = turn(v2_sb[i], (0, 1))
+            st[i]["b2"] = turn(st[i]["u"], (0, 1))
 
         def vt(i):
             if "vt" not in st[i]:
@@ -228,16 +228,16 @@ def tile_counterfactualfairnessabductiongap_x2_kernel(
                 )
 
         def u_op(i):
-            dst = ut(i)
-            turned = st[i]["b2"][:].rearrange("p g u n -> p (g u n)").bitcast(BF16)
-            turned = turned.rearrange("p (g u n e) -> p g n u e", g=2, u=2, e=2)
-            for k in range(2):
-                gain = g_col[:, k, :].rearrange("p (u e) -> p u e", e=2).unsqueeze(1).to_broadcast([P, P, 2, 2])
-                nc.vector.tensor_tensor(
-                    out=dst[:, 0, k].rearrange("p n (u e) -> p n u e", e=2), in0=turned[:, k], in1=gain, op=ALU.mult
-                )
+            st[i]["u"] = ahead.tile([P, F], BF16, name="u", align_bytes=64)
+            nc.vector.tensor_tensor(out=st[i]["u"][:], in0=v2_sb[i][:], in1=g_b[:], op=ALU.mult)
+
+        def ev2(i):
+            unload(st[i]["b2"], ut(i)[:, 0])
+
+        def qu(i):
             if i == NT - 1:
-                quant(st[i]["uq"][:, 0 : 2 * P], st[i]["us"][:, 0 : 2 * P], dst[:, 0].rearrange("p g n t -> p (g n t)"))
+                src = ut(i)[:, 0].rearrange("p g n t -> p (g n t)")
+                quant(st[i]["uq"][:, 0 : 2 * P], st[i]["us"][:, 0 : 2 * P], src)
 
         def tp3(i):
             if i == NT - 1:
@@ -309,43 +309,45 @@ def tile_counterfactualfairnessabductiongap_x2_kernel(
                     in_=groups[G]["s"][32 * q : 32 * q + 4, :].bitcast(I32),
                 )
 
-        for k in range(-4, NT + 4):
+        for k in range(-4, NT + 5):
 
             def at(offset, op, *args):
                 if 0 <= k - offset < NT:
                     op(k - offset, *args)
 
-            at(-1, ev1c)
+            at(1, m1, 1, 0)
             at(1, tanh, 1, 0)
-            at(4, m2, 0)
-            at(4, sig, 0)
             at(1, m1, 0, 0)
-            at(3, tp3)
-            at(3, ev3)
-            at(0, q1)
-            at(2, e_op)
-            at(-4, stt)
-            at(3, q2)
-            at(2, x_op)
             at(1, tanh, 0, 0)
             at(1, m1, 1, 1)
             at(1, tanh, 1, 1)
             at(1, m1, 0, 1)
             at(1, tanh, 0, 1)
-            at(4, m2, 1)
-            at(4, sig, 1)
-            at(4, df)
-            at(1, d_op)
-            at(-1, tp1)
-            at(-1, ev1)
-            at(2, tp2)
-            at(2, u_op)
+            at(5, m2, 1)
+            at(5, sig, 1)
+            at(-3, tp1)
+            at(-3, ev1)
+            at(-1, q1)
+            at(4, qu)
+            at(4, q2)
+            at(5, df)
+            at(0, u_op)
+            at(-4, stt)
+            at(3, tp2)
+            at(3, ev2)
             at(-2, tp1c)
-            at(0, m1, 1, 0)
-            if k in (8, 9):
-                pack(0, 256 * (k - 8), 256 * (k - 8) + 128, nc.scalar.copy)
-                pack(0, 256 * (k - 8) + 128, 256 * (k - 8) + 256, nc.scalar.copy)
-            if k == 10:
+            at(-2, ev1c)
+            at(3, tp3)
+            at(3, ev3)
+            at(4, m2, 0)
+            at(4, sig, 0)
+            at(2, e_op)
+            at(1, d_op)
+            at(2, x_op)
+            if k in (9, 10, 11):
+                for c in {9: (0, 1), 10: (2,), 11: (3,)}[k]:
+                    pack(0, 128 * c, 128 * c + 128, nc.scalar.copy)
+            if k == 12:
                 plane_words(0, 0, C)
                 plane_scales(0)
         pack(1, 0, 128, nc.scalar.copy)

@@ -87,19 +87,17 @@ def tile_counterfactualfairnessabductiongap_x2_kernel(
         load_v1(0)
         load_v1(1)
         load_weight(w_sb, w_sc, w_words, w_scales)
-        load_v2(0)
         load_v1(2)
         load_v1(3)
-        load_v2(1)
+        load_v2(0)
         load_v1(4)
-        load_v2(2)
-        load_weight(wy_sb, wy_sc, wy_words, wy_scales)
+        load_v2(1)
         load_v1(5)
-        load_v2(3)
-        load_v1(6)
-        load_v2(4)
-        load_v1(7)
-        for i in range(5, NT):
+        load_weight(wy_sb, wy_sc, wy_words, wy_scales)
+        for i in range(2, 4):
+            load_v2(i)
+            load_v1(i + 4)
+        for i in range(4, NT):
             load_v2(i)
 
         nc.vector.tensor_scalar(
@@ -151,7 +149,7 @@ def tile_counterfactualfairnessabductiongap_x2_kernel(
             st[i]["b1c"] = turn(st[i]["v1c"], (0, 1))
 
         def tp2(i):
-            st[i]["b2"] = turn(st[i]["u"], (0, 1))
+            st[i]["b2"] = turn(v2_sb[i], (0, 1))
 
         def vt(i):
             if "vt" not in st[i]:
@@ -198,41 +196,56 @@ def tile_counterfactualfairnessabductiongap_x2_kernel(
             st[i]["m1", which, half] = bank
 
         def tanh(i, which, half):
-            key = "hc" if which else "h"
-            if key not in st[i]:
-                st[i][key] = work.tile([P, F], F32, name=key)
-            nc.scalar.activation(
-                out=st[i][key][:, 512 * half : 512 * (half + 1)], in_=st[i]["m1", which, half][:], func=ACT.Tanh
-            )
-
-        def pieces(i):
-            return ((0, 512), (512, 1024)) if i == NT - 1 else ((0, 1024),)
+            t = work.tile([P, 512], F32, name="h%d%d" % (which, half), align_bytes=64)
+            bank = st[i]["m1", which, half]
+            if half == 0:
+                nc.scalar.activation(out=t[:], in_=bank[:], func=ACT.Tanh)
+            else:
+                nc.scalar.activation(
+                    out=t[:].rearrange("p (t m) -> p t m", t=4),
+                    in_=bank[:].rearrange("p (m t) -> p t m", t=4),
+                    func=ACT.Tanh,
+                )
+            st[i]["t", which, half] = t
 
         def d_op(i):
-            st[i]["e"] = work.tile([P, F], F32, name="e")
-            for lo, hi in pieces(i):
-                nc.vector.tensor_tensor(
-                    out=st[i]["e"][:, lo:hi], in0=st[i]["hc"][:, lo:hi], in1=st[i]["h"][:, lo:hi], op=ALU.subtract
-                )
+            st[i]["e"] = work.tile([P, 512], F32, name="e")
+            nc.vector.tensor_tensor(
+                out=st[i]["e"][:], in0=st[i]["t", 1, 0][:], in1=st[i]["t", 0, 0][:], op=ALU.subtract
+            )
 
         def e_op(i):
-            for lo, hi in pieces(i):
-                e = st[i]["e"][:, lo:hi]
-                nc.vector.tensor_tensor(out=e, in0=e, in1=v2_sb[i][:, lo:hi], op=ALU.add)
+            e = st[i]["e"][:]
+            nc.vector.tensor_tensor(out=e, in0=e, in1=v2_sb[i][:, 0:512], op=ALU.add)
 
         def x_op(i):
-            st[i]["uc"] = work.tile([P, F], BF16, name="uc", align_bytes=64)
-            for lo, hi in pieces(i):
-                nc.vector.tensor_tensor(
-                    out=st[i]["uc"][:, lo:hi], in0=st[i]["e"][:, lo:hi], in1=g_b[:, lo:hi], op=ALU.mult
-                )
+            st[i]["uc"] = work.tile([P, 512], BF16, name="uc", align_bytes=64)
+            nc.vector.tensor_tensor(out=st[i]["uc"][:], in0=st[i]["e"][:], in1=g_b[:, 0:512], op=ALU.mult)
+
+        def f_op(i):
+            f = work.tile([P, 4, P], F32, name="f")
+            nc.vector.tensor_tensor(
+                out=f[:],
+                in0=v2_sb[i][:, 512:1024].rearrange("p (m t) -> p t m", t=4),
+                in1=st[i]["t", 0, 1][:].rearrange("p (t m) -> p t m", t=4),
+                op=ALU.subtract,
+            )
+            st[i]["f"] = f
+
+        def gain(k):
+            return g_col[:, k, :].unsqueeze(1).to_broadcast([P, P, 4])
 
         def u_op(i):
-            st[i]["u"] = ahead.tile([P, F], BF16, name="u", align_bytes=64)
-            nc.vector.tensor_tensor(out=st[i]["u"][:], in0=v2_sb[i][:], in1=g_b[:], op=ALU.mult)
-
-        def ev2(i):
-            unload(st[i]["b2"], ut(i)[:, 0])
+            dst = ut(i)
+            turned = st[i]["b2"][:].rearrange("p g u n -> p (g u n)").bitcast(BF16)
+            turned = turned.rearrange("p (g u n e) -> p g n u e", g=2, u=2, e=2)
+            for k in range(2):
+                nc.vector.tensor_tensor(
+                    out=dst[:, 0, k].rearrange("p n (u e) -> p n u e", e=2),
+                    in0=turned[:, k],
+                    in1=g_col[:, k, :].rearrange("p (u e) -> p u e", e=2).unsqueeze(1).to_broadcast([P, P, 2, 2]),
+                    op=ALU.mult,
+                )
 
         def qu(i):
             if i == NT - 1:
@@ -240,18 +253,27 @@ def tile_counterfactualfairnessabductiongap_x2_kernel(
                 quant(st[i]["uq"][:, 0 : 2 * P], st[i]["us"][:, 0 : 2 * P], src)
 
         def tp3(i):
-            if i == NT - 1:
-                st[i]["b3"] = [turn(st[i]["uc"], (k,)) for k in range(2)]
-            else:
-                st[i]["b3"] = [turn(st[i]["uc"], (0, 1))]
+            st[i]["b3"] = turn(st[i]["uc"], (0,))
 
         def ev3(i):
-            dst = ut(i)
-            if i == NT - 1:
-                for k in range(2):
-                    unload(st[i]["b3"][k], dst[:, 1, k : k + 1])
-            else:
-                unload(st[i]["b3"][0], dst[:, 1])
+            unload(st[i]["b3"], ut(i)[:, 1, 0:1])
+
+        def tp4(i):
+            bank = tp_pool.tile([P, 4, P], F32, name="summed", tag="tp")
+            hc = st[i]["t", 1, 1][:].rearrange("p (t m) -> p t m", t=4)
+            for t in range(4):
+                nc.tensor.matmul(
+                    out=bank[:, t, :], lhsT=st[i]["f"][:, t, :], rhs=ident[:], is_transpose=True, start=True, stop=False
+                )
+                nc.tensor.matmul(
+                    out=bank[:, t, :], lhsT=hc[:, t, :], rhs=ident[:], is_transpose=True, start=False, stop=True
+                )
+            st[i]["b4"] = bank
+
+        def y_op(i):
+            nc.vector.tensor_tensor(
+                out=ut(i)[:, 1, 1], in0=st[i]["b4"][:].rearrange("p t n -> p n t"), in1=gain(1), op=ALU.mult
+            )
 
         def q2(i):
             t = ut(i)
@@ -309,44 +331,46 @@ def tile_counterfactualfairnessabductiongap_x2_kernel(
                     in_=groups[G]["s"][32 * q : 32 * q + 4, :].bitcast(I32),
                 )
 
-        for k in range(-4, NT + 5):
+        for k in range(-3, NT + 6):
 
             def at(offset, op, *args):
                 if 0 <= k - offset < NT:
                     op(k - offset, *args)
 
-            at(1, m1, 1, 0)
             at(1, tanh, 1, 0)
-            at(1, m1, 0, 0)
-            at(1, tanh, 0, 0)
-            at(1, m1, 1, 1)
-            at(1, tanh, 1, 1)
-            at(1, m1, 0, 1)
-            at(1, tanh, 0, 1)
+            at(2, tanh, 0, 1)
+            at(5, m2, 0)
             at(5, m2, 1)
-            at(5, sig, 1)
+            at(5, sig, 0)
             at(-3, tp1)
             at(-3, ev1)
-            at(-1, q1)
-            at(4, qu)
-            at(4, q2)
-            at(5, df)
-            at(0, u_op)
-            at(-4, stt)
-            at(3, tp2)
-            at(3, ev2)
             at(-2, tp1c)
             at(-2, ev1c)
+            at(5, sig, 1)
+            at(2, tp2)
+            at(3, tp4)
             at(3, tp3)
             at(3, ev3)
-            at(4, m2, 0)
-            at(4, sig, 0)
+            at(1, m1, 1, 1)
+            at(1, tanh, 1, 1)
+            at(0, m1, 0, 0)
+            at(0, tanh, 0, 0)
+            at(0, m1, 1, 0)
+            at(1, m1, 0, 1)
+            at(3, u_op)
+            at(6, df)
+            at(-3, stt)
+            at(4, y_op)
             at(2, e_op)
-            at(1, d_op)
+            at(-1, q1)
             at(2, x_op)
-            if k in (9, 10, 11):
-                for c in {9: (0, 1), 10: (2,), 11: (3,)}[k]:
-                    pack(0, 128 * c, 128 * c + 128, nc.scalar.copy)
+            at(4, q2)
+            at(1, d_op)
+            at(2, f_op)
+            at(3, qu)
+            if k in (10, 11):
+                pack(0, 256 * (k - 10), 256 * (k - 10) + 128, nc.scalar.copy)
+                pack(0, 256 * (k - 10) + 128, 256 * (k - 10) + 256, nc.scalar.copy)
             if k == 12:
                 plane_words(0, 0, C)
                 plane_scales(0)

@@ -45,7 +45,7 @@ def tile_counterfactualfairnessabductiongap_x2_kernel(
         s_col = keep.tile([P, 2, 4], BF16, name="s_col")
         m2s = keep.tile([P, NT], F32, name="m2s")
         a_b = keep.tile([P, D], BF16, name="a_b", align_bytes=64)
-        g_b = keep.tile([P, F], BF16, name="g_b", align_bytes=64)
+        g_b = keep.tile([P, 512], BF16, name="g_b", align_bytes=64)
         warm = keep.tile([P, 1], F32, name="warm")
 
         v1_rows = v1.rearrange("(g m t) d -> g t m d", m=P, t=4)
@@ -104,35 +104,47 @@ def tile_counterfactualfairnessabductiongap_x2_kernel(
             out=m2s[:], in0=s_col[:].rearrange("p g t -> p (g t)"), scalar1=-2.0, scalar2=None, op0=ALU.mult
         )
 
-        def spread(col, full, copy):
-            bank = tp_pool.tile([P, NT, P], BF16, name="spread", tag="tp")
+        def spread(col, full, n, copy):
+            bank = tp_pool.tile([P, n, P], BF16, name="spread", tag="tp")
             flat = col[:].rearrange("p g t -> p (g t)")
-            for j in range(8):
+            for j in range(n):
                 nc.tensor.transpose(bank[:, j, :], flat[:, j : j + 1].to_broadcast([P, P]), ident_bf[:])
             copy(
-                out=full[:].rearrange("p (g n t) -> p g n t", g=2, t=4),
-                in_=bank[:].rearrange("p (g t) n -> p g n t", g=2),
+                out=full[:].rearrange("p (q m e) -> p q m e", m=P, e=2),
+                in_=bank[:].rearrange("p (q e) m -> p q m e", e=2),
             )
 
-        spread(a_col, a_b, nc.vector.tensor_copy)
-        spread(g_col, g_b, nc.scalar.copy)
+        spread(a_col, a_b, 8, nc.vector.tensor_copy)
+        spread(g_col, g_b, 4, nc.scalar.copy)
 
         st = [dict() for i in range(NT)]
         groups = [dict(), dict()]
 
+        def r1(i):
+            t = ahead.tile([P, D], BF16, name="v1r", align_bytes=64)
+            nc.scalar.copy(
+                out=t[:].bitcast(F32).rearrange("p (g u m) -> p g u m", g=2, u=2),
+                in_=v1_sb[i][:].bitcast(F32).rearrange("p (g m u) -> p g u m", g=2, u=2),
+            )
+            st[i]["v1r"] = t
+
         def stt(i):
             t = ahead.tile([P, D], BF16, name="v1c", align_bytes=64)
             nc.vector.scalar_tensor_tensor(
-                out=t[:], in0=a_b[:], scalar=m2s[:, i : i + 1], in1=v1_sb[i][:], op0=ALU.mult, op1=ALU.add
+                out=t[:], in0=a_b[:], scalar=m2s[:, i : i + 1], in1=st[i]["v1r"][:], op0=ALU.mult, op1=ALU.add
             )
             st[i]["v1c"] = t
 
-        def turn(src, ks):
+        def turn(src, ks, apart):
             words = src[:].bitcast(F32)
             bank = tp_pool.tile([P, len(ks), 2, P], F32, name="turned", tag="tp")
             for j, k in enumerate(ks):
                 for u in range(2):
-                    nc.tensor.transpose(bank[:, j, u, :], words[:, 256 * k + u : 256 * (k + 1) : 2], ident[:])
+                    if apart:
+                        cols = slice(256 * k + 128 * u, 256 * k + 128 * (u + 1))
+                    else:
+                        cols = slice(256 * k + u, 256 * (k + 1), 2)
+                    nc.tensor.transpose(bank[:, j, u, :], words[:, cols], ident[:])
             return bank
 
         def unload(bank, dst):
@@ -143,13 +155,13 @@ def tile_counterfactualfairnessabductiongap_x2_kernel(
             )
 
         def tp1(i):
-            st[i]["b1"] = turn(v1_sb[i], (0, 1))
+            st[i]["b1"] = turn(st[i]["v1r"], (0, 1), True)
 
         def tp1c(i):
-            st[i]["b1c"] = turn(st[i]["v1c"], (0, 1))
+            st[i]["b1c"] = turn(st[i]["v1c"], (0, 1), True)
 
         def tp2(i):
-            st[i]["b2"] = turn(v2_sb[i], (0, 1))
+            st[i]["b2"] = turn(v2_sb[i], (0, 1), False)
 
         def vt(i):
             if "vt" not in st[i]:
@@ -172,10 +184,20 @@ def tile_counterfactualfairnessabductiongap_x2_kernel(
         def quant(codes, scales, src):
             nc.vector.quantize_mx(out=codes.bitcast(FP8X4), scales=scales, in_=src)
 
+        def quant_v(i, whichs):
+            if "vq" not in st[i]:
+                st[i]["vq"] = work.tile([P, 4 * P], U32, name="vq", align_bytes=64)
+                st[i]["vs"] = work.tile([P, 4 * P], U8, name="vs", align_bytes=64)
+            lo, hi = whichs
+            cols = slice(2 * P * lo, 2 * P * hi)
+            quant(st[i]["vq"][:, cols], st[i]["vs"][:, cols], vt(i)[:, lo:hi].rearrange("p w g n t -> p (w g n t)"))
+
+        def qa(i):
+            if i == 0:
+                quant_v(i, (0, 1))
+
         def q1(i):
-            st[i]["vq"] = work.tile([P, 4 * P], U32, name="vq", align_bytes=64)
-            st[i]["vs"] = work.tile([P, 4 * P], U8, name="vs", align_bytes=64)
-            quant(st[i]["vq"][:], st[i]["vs"][:], vt(i)[:].rearrange("p w g n t -> p (w g n t)"))
+            quant_v(i, (1, 2) if i == 0 else (0, 2))
 
         def mx(bank, codes, scales, first, words, wscales, half):
             for k in range(2):
@@ -220,7 +242,12 @@ def tile_counterfactualfairnessabductiongap_x2_kernel(
 
         def x_op(i):
             st[i]["uc"] = work.tile([P, 512], BF16, name="uc", align_bytes=64)
-            nc.vector.tensor_tensor(out=st[i]["uc"][:], in0=st[i]["e"][:], in1=g_b[:, 0:512], op=ALU.mult)
+            nc.vector.tensor_tensor(
+                out=st[i]["uc"][:].rearrange("p (u m e) -> p u m e", u=2, e=2),
+                in0=st[i]["e"][:].rearrange("p (m u e) -> p u m e", u=2, e=2),
+                in1=g_b[:].rearrange("p (u m e) -> p u m e", u=2, e=2),
+                op=ALU.mult,
+            )
 
         def f_op(i):
             f = work.tile([P, 4, P], F32, name="f")
@@ -253,7 +280,7 @@ def tile_counterfactualfairnessabductiongap_x2_kernel(
                 quant(st[i]["uq"][:, 0 : 2 * P], st[i]["us"][:, 0 : 2 * P], src)
 
         def tp3(i):
-            st[i]["b3"] = turn(st[i]["uc"], (0,))
+            st[i]["b3"] = turn(st[i]["uc"], (0,), True)
 
         def ev3(i):
             unload(st[i]["b3"], ut(i)[:, 1, 0:1])
@@ -331,46 +358,48 @@ def tile_counterfactualfairnessabductiongap_x2_kernel(
                     in_=groups[G]["s"][32 * q : 32 * q + 4, :].bitcast(I32),
                 )
 
-        for k in range(-3, NT + 6):
+        for k in range(-4, NT + 6):
 
             def at(offset, op, *args):
                 if 0 <= k - offset < NT:
                     op(k - offset, *args)
 
             at(1, tanh, 1, 0)
-            at(2, tanh, 0, 1)
-            at(5, m2, 0)
-            at(5, m2, 1)
-            at(5, sig, 0)
-            at(-3, tp1)
-            at(-3, ev1)
-            at(-2, tp1c)
-            at(-2, ev1c)
-            at(5, sig, 1)
-            at(2, tp2)
-            at(3, tp4)
-            at(3, tp3)
-            at(3, ev3)
-            at(1, m1, 1, 1)
-            at(1, tanh, 1, 1)
-            at(0, m1, 0, 0)
-            at(0, tanh, 0, 0)
-            at(0, m1, 1, 0)
-            at(1, m1, 0, 1)
-            at(3, u_op)
-            at(6, df)
-            at(-3, stt)
-            at(4, y_op)
-            at(2, e_op)
-            at(-1, q1)
-            at(2, x_op)
-            at(4, q2)
+            at(2, tanh, 1, 1)
+            at(-2, ev1)
+            at(6, sig, 0)
+            at(-1, ev1c)
             at(1, d_op)
+            at(-3, stt)
+            at(3, u_op)
+            at(-2, qa)
+            at(4, y_op)
+            at(-1, q1)
+            at(1, e_op)
+            at(4, qu)
+            at(-2, tp1c)
+            at(2, tp2)
+            at(-1, m1, 0, 0)
+            at(1, m1, 0, 1)
+            at(5, m2, 1)
+            at(3, tp3)
+            at(3, tp4)
+            at(-1, m1, 1, 0)
+            at(0, tanh, 0, 0)
+            at(2, tanh, 0, 1)
+            at(4, ev3)
+            at(6, sig, 1)
+            at(6, df)
             at(2, f_op)
-            at(3, qu)
-            if k in (10, 11):
-                pack(0, 256 * (k - 10), 256 * (k - 10) + 128, nc.scalar.copy)
-                pack(0, 256 * (k - 10) + 128, 256 * (k - 10) + 256, nc.scalar.copy)
+            at(4, q2)
+            at(2, x_op)
+            at(4, m2, 0)
+            at(0, m1, 1, 1)
+            at(-4, r1)
+            at(-4, tp1)
+            if k in (10, 11, 12):
+                for c in {10: (0, 1), 11: (2,), 12: (3,)}[k]:
+                    pack(0, 128 * c, 128 * c + 128, nc.scalar.copy)
             if k == 12:
                 plane_words(0, 0, C)
                 plane_scales(0)

from contextlib import ExitStack

import concourse.mybir as mybir
from concourse.masks import make_identity

F32 = mybir.dt.float32
BF16 = mybir.dt.bfloat16
I32 = mybir.dt.int32
U32 = mybir.dt.uint32
U8 = mybir.dt.uint8
FP8X4 = mybir.dt.float8_e4m3fn_x4
FP4X4 = mybir.dt.float4_e2m1fn_x4
ALU = mybir.AluOpType
ACT = mybir.ActivationFunctionType

N, D, F, C = 1024, 1024, 1024, 512
P = 128
NT = N // P
FLOPS = 2 * (2 * N * D * F) + 2 * (2 * N * F * C)


def tile_counterfactualfairnessabductiongap_x2_kernel(
    tc, v1, v2, s, a, w_words, w_scales, g, wy_words, wy_scales, out_0, out_1, out_2
):
    nc = tc.nc
    with ExitStack() as ctx:
        keep = ctx.enter_context(tc.tile_pool(name="keep", bufs=1))
        inp = ctx.enter_context(tc.tile_pool(name="inp", bufs=NT))
        ahead = ctx.enter_context(tc.tile_pool(name="ahead", bufs=6))
        work = ctx.enter_context(tc.tile_pool(name="work", bufs=4))
        res = ctx.enter_context(tc.tile_pool(name="res", bufs=2))
        tp_pool = ctx.enter_context(tc.psum_pool(name="tp", bufs=3))
        m1_pool = ctx.enter_context(tc.psum_pool(name="m1", bufs=3))
        m2_pool = ctx.enter_context(tc.psum_pool(name="m2", bufs=2))
        ctx.enter_context(tc.manual_schedule())

        ident = keep.tile([P, P], F32, name="ident")
        ident_bf = keep.tile([P, P], BF16, name="ident_bf")
        w_sb = keep.tile([P, 2, 2 * F], U8, name="w_sb", align_bytes=64)
        w_sc = keep.tile([P, 2, F], U8, name="w_sc", align_bytes=64)
        wy_sb = keep.tile([P, 2, 2 * C], U8, name="wy_sb", align_bytes=64)
        wy_sc = keep.tile([P, 2, C], U8, name="wy_sc", align_bytes=64)
        a_col = keep.tile([P, 2, 4], BF16, name="a_col")
        g_col = keep.tile([P, 2, 4], BF16, name="g_col")
        s_col = keep.tile([P, 2, 4], BF16, name="s_col")
        m2s = keep.tile([P, NT], F32, name="m2s")
        a_b = keep.tile([P, D], BF16, name="a_b", align_bytes=64)
        g_b = keep.tile([P, 512], BF16, name="g_b", align_bytes=64)
        warm = keep.tile([P, 1], F32, name="warm")

        v1_rows = v1.rearrange("(g m t) d -> g t m d", m=P, t=4)
        v2_rows = v2.rearrange("(g m t) d -> g t m d", m=P, t=4)
        out_rows = out_0.rearrange("(g m t) c -> g t m c", m=P, t=4)

        make_identity(nc, ident_bf[:])
        make_identity(nc, ident[:])
        nc.vector.memset(w_sc[:].rearrange("p g n -> p (g n)").bitcast(I32), 0)
        nc.vector.memset(wy_sc[:].rearrange("p g n -> p (g n)").bitcast(I32), 0)

        for queue, col, src in ((nc.sync, a_col, a), (nc.scalar, s_col, s), (nc.scalar, g_col, g)):
            queue.dma_start(out=col[:], in_=src.rearrange("(g p t) -> p g t", p=P, t=4))
        nc.vector.memset(warm[:], 0.0)
        nc.scalar.activation(out=warm[:], in_=warm[:], func=ACT.Sigmoid)

        v1_sb, v2_sb = [], []
        for i in range(NT):
            v1_sb.append(inp.tile([P, D], BF16, name="v1_t", align_bytes=64))
            v2_sb.append(inp.tile([P, F], BF16, name="v2_t", align_bytes=64))

        def load_v1(i):
            nc.sync.dma_start(out=v1_sb[i][:], in_=v1_rows[i // 4, i % 4])

        def load_v2(i):
            nc.sync.dma_start(out=v2_sb[i][:], in_=v2_rows[i // 4, i % 4])

        def load_weight(words_sb, scales_sb, words, scales):
            rows = scales.bitcast(I32)
            plane = scales_sb[:].bitcast(I32)
            for q in range(4):
                nc.sync.dma_start(
                    out=plane[32 * q : 32 * q + 4],
                    in_=rows[:, 4 * q : 4 * q + 4, :].rearrange("g r n -> r g n"),
                )
            for k in range(2):
                nc.sync.dma_start(out=words_sb[:, k, :].bitcast(I32), in_=words[k].bitcast(I32))

        load_v1(0)
        load_v1(1)
        load_weight(w_sb, w_sc, w_words, w_scales)
        load_v1(2)
        load_v1(3)
        load_v2(0)
        load_v1(4)
        load_v2(1)
        load_v1(5)
        load_weight(wy_sb, wy_sc, wy_words, wy_scales)
        for i in range(2, 4):
            load_v2(i)
            load_v1(i + 4)
        for i in range(4, NT):
            load_v2(i)

        nc.vector.tensor_scalar(
            out=m2s[:], in0=s_col[:].rearrange("p g t -> p (g t)"), scalar1=-2.0, scalar2=None, op0=ALU.mult
        )

        def spread(col, full, n, copy):
            bank = tp_pool.tile([P, n, P], BF16, name="spread", tag="tp")
            flat = col[:].rearrange("p g t -> p (g t)")
            for j in range(n):
                nc.tensor.transpose(bank[:, j, :], flat[:, j : j + 1].to_broadcast([P, P]), ident_bf[:])
            copy(
                out=full[:].rearrange("p (q m e) -> p q m e", m=P, e=2),
                in_=bank[:].rearrange("p (q e) m -> p q m e", e=2),
            )

        spread(a_col, a_b, 8, nc.vector.tensor_copy)
        spread(g_col, g_b, 4, nc.scalar.copy)

        st = [dict() for i in range(NT)]
        groups = [dict(), dict()]

        def r1(i):
            t = ahead.tile([P, D], BF16, name="v1r", align_bytes=64)
            nc.scalar.copy(
                out=t[:].bitcast(F32).rearrange("p (g u m) -> p g u m", g=2, u=2),
                in_=v1_sb[i][:].bitcast(F32).rearrange("p (g m u) -> p g u m", g=2, u=2),
            )
            st[i]["v1r"] = t

        def stt(i):
            t = ahead.tile([P, D], BF16, name="v1c", align_bytes=64)
            nc.vector.scalar_tensor_tensor(
                out=t[:], in0=a_b[:], scalar=m2s[:, i : i + 1], in1=st[i]["v1r"][:], op0=ALU.mult, op1=ALU.add
            )
            st[i]["v1c"] = t

        def turn(src, ks, apart):
            words = src[:].bitcast(F32)
            bank = tp_pool.tile([P, len(ks), 2, P], F32, name="turned", tag="tp")
            for j, k in enumerate(ks):
                for u in range(2):
                    if apart:
                        cols = slice(256 * k + 128 * u, 256 * k + 128 * (u + 1))
                    else:
                        cols = slice(256 * k + u, 256 * (k + 1), 2)
                    nc.tensor.transpose(bank[:, j, u, :], words[:, cols], ident[:])
            return bank

        def unload(bank, dst):
            k = dst.shape[1]
            nc.scalar.copy(
                out=dst.rearrange("p g n t -> p (g n t)").bitcast(F32).rearrange("p (g n u) -> p g n u", g=k, u=2),
                in_=bank[:].rearrange("p g u n -> p g n u"),
            )

        def tp1(i):
            st[i]["b1"] = turn(st[i]["v1r"], (0, 1), True)

        def tp1c(i):
            st[i]["b1c"] = turn(st[i]["v1c"], (0, 1), True)

        def tp2(i):
            st[i]["b2"] = turn(v2_sb[i], (0, 1), False)

        def vt(i):
            if "vt" not in st[i]:
                st[i]["vt"] = work.tile([P, 2, 2, P, 4], BF16, name="vt", align_bytes=64)
            return st[i]["vt"]

        def ut(i):
            if "ut" not in st[i]:
                st[i]["ut"] = work.tile([P, 2, 2, P, 4], BF16, name="ut", align_bytes=64)
                st[i]["uq"] = work.tile([P, 4 * P], U32, name="uq", align_bytes=64)
                st[i]["us"] = work.tile([P, 4 * P], U8, name="us", align_bytes=64)
            return st[i]["ut"]

        def ev1(i):
            unload(st[i]["b1"], vt(i)[:, 0])

        def ev1c(i):
            unload(st[i]["b1c"], vt(i)[:, 1])

        def quant(codes, scales, src):
            nc.vector.quantize_mx(out=codes.bitcast(FP8X4), scales=scales, in_=src)

        def quant_v(i, whichs):
            if "vq" not in st[i]:
                st[i]["vq"] = work.tile([P, 4 * P], U32, name="vq", align_bytes=64)
                st[i]["vs"] = work.tile([P, 4 * P], U8, name="vs", align_bytes=64)
            lo, hi = whichs
            cols = slice(2 * P * lo, 2 * P * hi)
            quant(st[i]["vq"][:, cols], st[i]["vs"][:, cols], vt(i)[:, lo:hi].rearrange("p w g n t -> p (w g n t)"))

        def qa(i):
            if i == 0:
                quant_v(i, (0, 1))

        def q1(i):
            quant_v(i, (1, 2) if i == 0 else (0, 2))

        def mx(bank, codes, scales, first, words, wscales, half):
            for k in range(2):
                cols = slice((first + k) * P, (first + k + 1) * P)
                nc.tensor.matmul_mx(
                    out=bank[:],
                    lhsT=codes[:, cols].bitcast(FP8X4),
                    lhsT_scale=scales[:, cols],
                    rhs=words[:, k, 1024 * half : 1024 * (half + 1)].bitcast(FP4X4),
                    rhs_scale=wscales[:, k, 512 * half : 512 * (half + 1)],
                    start=(k == 0),
                    stop=(k == 1),
                )

        def m1(i, which, half):
            bank = m1_pool.tile([P, 512], F32, name="m1", tag="m1")
            mx(bank, st[i]["vq"], st[i]["vs"], 2 * which, w_sb, w_sc, half)
            st[i]["m1", which, half] = bank

        def tanh(i, which, half):
            t = work.tile([P, 512], F32, name="h%d%d" % (which, half), align_bytes=64)
            bank = st[i]["m1", which, half]
            if half == 0:
                nc.scalar.activation(out=t[:], in_=bank[:], func=ACT.Tanh)
            else:
                nc.scalar.activation(
                    out=t[:].rearrange("p (t m) -> p t m", t=4),
                    in_=bank[:].rearrange("p (m t) -> p t m", t=4),
                    func=ACT.Tanh,
                )
            st[i]["t", which, half] = t

        def d_op(i):
            st[i]["e"] = work.tile([P, 512], F32, name="e")
            nc.vector.tensor_tensor(
                out=st[i]["e"][:], in0=st[i]["t", 1, 0][:], in1=st[i]["t", 0, 0][:], op=ALU.subtract
            )

        def e_op(i):
            e = st[i]["e"][:]
            nc.vector.tensor_tensor(out=e, in0=e, in1=v2_sb[i][:, 0:512], op=ALU.add)

        def x_op(i):
            st[i]["uc"] = work.tile([P, 512], BF16, name="uc", align_bytes=64)
            nc.vector.tensor_tensor(
                out=st[i]["uc"][:].rearrange("p (u m e) -> p u m e", u=2, e=2),
                in0=st[i]["e"][:].rearrange("p (m u e) -> p u m e", u=2, e=2),
                in1=g_b[:].rearrange("p (u m e) -> p u m e", u=2, e=2),
                op=ALU.mult,
            )

        def f_op(i):
            f = work.tile([P, 4, P], F32, name="f")
            nc.vector.tensor_tensor(
                out=f[:],
                in0=v2_sb[i][:, 512:1024].rearrange("p (m t) -> p t m", t=4),
                in1=st[i]["t", 0, 1][:].rearrange("p (t m) -> p t m", t=4),
                op=ALU.subtract,
            )
            st[i]["f"] = f

        def gain(k):
            return g_col[:, k, :].unsqueeze(1).to_broadcast([P, P, 4])

        def u_op(i):
            dst = ut(i)
            turned = st[i]["b2"][:].rearrange("p g u n -> p (g u n)").bitcast(BF16)
            turned = turned.rearrange("p (g u n e) -> p g n u e", g=2, u=2, e=2)
            for k in range(2):
                nc.vector.tensor_tensor(
                    out=dst[:, 0, k].rearrange("p n (u e) -> p n u e", e=2),
                    in0=turned[:, k],
                    in1=g_col[:, k, :].rearrange("p (u e) -> p u e", e=2).unsqueeze(1).to_broadcast([P, P, 2, 2]),
                    op=ALU.mult,
                )

        def qu(i):
            if i == NT - 1:
                src = ut(i)[:, 0].rearrange("p g n t -> p (g n t)")
                quant(st[i]["uq"][:, 0 : 2 * P], st[i]["us"][:, 0 : 2 * P], src)

        def tp3(i):
            st[i]["b3"] = turn(st[i]["uc"], (0,), True)

        def ev3(i):
            unload(st[i]["b3"], ut(i)[:, 1, 0:1])

        def tp4(i):
            bank = tp_pool.tile([P, 4, P], F32, name="summed", tag="tp")
            hc = st[i]["t", 1, 1][:].rearrange("p (t m) -> p t m", t=4)
            for t in range(4):
                nc.tensor.matmul(
                    out=bank[:, t, :], lhsT=st[i]["f"][:, t, :], rhs=ident[:], is_transpose=True, start=True, stop=False
                )
                nc.tensor.matmul(
                    out=bank[:, t, :], lhsT=hc[:, t, :], rhs=ident[:], is_transpose=True, start=False, stop=True
                )
            st[i]["b4"] = bank

        def y_op(i):
            nc.vector.tensor_tensor(
                out=ut(i)[:, 1, 1], in0=st[i]["b4"][:].rearrange("p t n -> p n t"), in1=gain(1), op=ALU.mult
            )

        def q2(i):
            t = ut(i)
            if i == NT - 1:
                for k in range(2):
                    cols = slice((2 + k) * P, (3 + k) * P)
                    quant(st[i]["uq"][:, cols], st[i]["us"][:, cols], t[:, 1, k].rearrange("p n t -> p (n t)"))
            else:
                quant(st[i]["uq"][:], st[i]["us"][:], t[:].rearrange("p w g n t -> p (w g n t)"))

        def m2(i, which):
            bank = m2_pool.tile([P, C], F32, name="m2", tag="m2")
            mx(bank, st[i]["uq"], st[i]["us"], 2 * which, wy_sb, wy_sc, 0)
            st[i]["m2", which] = bank

        def halves(i):
            return ((0, 256), (256, 512)) if i == NT - 1 else ((0, 512),)

        def sig(i, which):
            st[i]["p", which] = work.tile([P, C], F32, name="pc" if which else "p")
            for lo, hi in halves(i) if which else ((0, C),):
                nc.scalar.activation(
                    out=st[i]["p", which][:, lo:hi], in_=st[i]["m2", which][:, lo:hi], func=ACT.Sigmoid
                )

        def df(i):
            grp = groups[i // 4]
            if "r" not in grp:
                grp["r"] = res.tile([P, 4, C], F32, name="r")
                grp["pb"] = res.tile([P, C, 4], BF16, name="pb", align_bytes=64)
                grp["q"] = res.tile([P, C], U32, name="rq", align_bytes=64)
                grp["s"] = res.tile([P, C], U8, name="rs", align_bytes=64)
            for lo, hi in halves(i):
                r = grp["r"][:, i % 4, lo:hi]
                nc.vector.tensor_tensor(
                    out=r, in0=st[i]["p", 1][:, lo:hi], in1=st[i]["p", 0][:, lo:hi], op=ALU.subtract
                )
                nc.sync.dma_start(out=out_rows[i // 4, i % 4][:, lo:hi], in_=r)

        def pack(G, lo, hi, copy):
            grp = groups[G]
            copy(out=grp["pb"][:, lo:hi, :], in_=grp["r"][:, :, lo:hi].rearrange("p t c -> p c t"))

        def plane_words(G, lo, hi):
            grp = groups[G]
            quant(grp["q"][:, lo:hi], grp["s"][:, lo:hi], grp["pb"][:, lo:hi, :].rearrange("p c t -> p (c t)"))
            nc.sync.dma_start(
                out=out_1[G].rearrange("p m t -> p (m t)").bitcast(I32)[:, lo:hi], in_=grp["q"][:, lo:hi].bitcast(I32)
            )

        def plane_scales(G):
            for q in range(4):
                nc.sync.dma_start(
                    out=out_2[G, 4 * q : 4 * q + 4, :].bitcast(I32),
                    in_=groups[G]["s"][32 * q : 32 * q + 4, :].bitcast(I32),
                )

        for k in range(-4, NT + 6):

            def at(offset, op, *args):
                if 0 <= k - offset < NT:
                    op(k - offset, *args)

            at(1, tanh, 1, 0)
            at(2, tanh, 1, 1)
            at(-2, ev1)
            at(6, sig, 0)
            at(-1, ev1c)
            at(1, d_op)
            at(-3, stt)
            at(3, u_op)
            at(-2, qa)
            at(4, y_op)
            at(-1, q1)
            at(1, e_op)
            at(4, qu)
            at(-2, tp1c)
            at(2, tp2)
            at(-1, m1, 0, 0)
            at(1, m1, 0, 1)
            at(5, m2, 1)
            at(3, tp3)
            at(3, tp4)
            at(-1, m1, 1, 0)
            at(0, tanh, 0, 0)
            at(2, tanh, 0, 1)
            at(4, ev3)
            at(6, sig, 1)
            at(6, df)
            at(2, f_op)
            at(4, q2)
            at(2, x_op)
            at(4, m2, 0)
            at(0, m1, 1, 1)
            at(-4, r1)
            at(-4, tp1)
            if k in (10, 11, 12):
                for c in {10: (0, 1), 11: (2,), 12: (3,)}[k]:
                    pack(0, 128 * c, 128 * c + 128, nc.scalar.copy)
            if k == 12:
                plane_words(0, 0, C)
                plane_scales(0)
        pack(1, 0, 128, nc.scalar.copy)
        pack(1, 384, 512, nc.scalar.copy)
        pack(1, 128, 256, nc.vector.tensor_copy)
        plane_words(1, 0, 256)
        pack(1, 256, 384, nc.vector.tensor_copy)
        plane_words(1, 256, 512)
        plane_scales(1)
